import numpy as np
import ml_dtypes


def mxq(x, axis, fmt="e4m3"):
    dtype, down = {"e4m3": (ml_dtypes.float8_e4m3fn, 7), "e5m2": (ml_dtypes.float8_e5m2, 14)}[fmt]
    v = np.moveaxis(np.asarray(x, np.float32).astype(ml_dtypes.bfloat16).astype(np.float64), axis, -1)
    blocks = v.reshape(v.shape[:-1] + (-1, 32))
    amax = np.abs(blocks).max(-1, keepdims=True)
    byte = np.maximum(np.where(amax > 0, np.frexp(amax)[1] - 1 + 127, 0) - down, 1)
    scale = np.exp2(byte - 127.0)
    codes = (blocks / scale).astype(np.float32).astype(dtype).astype(np.float64)
    return np.moveaxis((codes * scale).reshape(v.shape), -1, axis)


WIDE = False


def mx_kscale(k):
    if not WIDE:
        return np.ones(k)
    levels = np.array([10, -10, 5, -5, 0])
    if k % 512:
        return np.exp2(np.random.permutation(np.resize(levels, k // 32))).repeat(32)
    a = np.empty((k // 512, 16))
    for p in range(k // 512):
        a[p, :8] = np.random.permutation(np.resize(levels, 8))
        for g in range(8):
            far = levels[np.abs(levels - a[p, g]) >= 10]
            a[p, g + 8] = far[np.random.randint(len(far))]
    return np.exp2(a.ravel()).repeat(32)


def f64(x):
    return np.asarray(x).astype(np.float64)


def striped(idx):
    return np.tile(idx.reshape(-1, 16).T, (8, 1)).astype(np.uint16)


def unstriped(offs):
    return offs[:16].T.reshape(-1).astype(np.int64)


def striped8(idx):
    return np.concatenate([x.reshape(-1, 16).T for x in idx]).astype(np.uint16)


def runs(offs, k):
    lists = np.stack([offs[16 * r : 16 * r + 16].T.reshape(-1) for r in range(8)]).astype(np.int64)
    return lists[np.arange(k) % 512 // 64]


def pack_weight(w):
    k, n = w.shape
    w = f64(np.asarray(w, np.float32).astype(ml_dtypes.bfloat16)).reshape(k // 32, 32, n)
    amax = np.abs(w).max(1)
    byte = np.clip(np.where(amax > 0, np.frexp(amax)[1] - 1 + 127 - 7, 1), 1, 254)
    scaled = (w * np.exp2(127.0 - byte)[:, None, :]).reshape(k, n).astype(np.float32)
    words = np.ascontiguousarray(scaled.reshape(k // 512, 128, 4, n).transpose(0, 1, 3, 2)).astype(ml_dtypes.float8_e4m3fn).view(np.uint8)
    return words, np.ascontiguousarray(byte.astype(np.uint8).reshape(k // 512, 16, n))


def unpack_weight(words, scales):
    g, p, n, _ = words.shape
    vals = np.ascontiguousarray(words).view(ml_dtypes.float8_e4m3fn).astype(np.float64) * np.repeat(np.exp2(scales.astype(np.float64) - 127.0), 8, axis=1)[..., None]
    return vals.transpose(0, 1, 3, 2).reshape(g * 512, n)

def planes(y):
    n, m = y.shape
    v = y.astype(np.float32).astype(ml_dtypes.bfloat16).astype(np.float64).reshape(n // 32, 32, m)
    top = np.abs(v).max(1)
    byte = np.clip(np.where(top > 0, np.frexp(top)[1] - 1 + 127 - 7, 1), 1, 254)
    codes = (v * np.exp2(127.0 - byte)[:, None, :]).reshape(n, m).astype(np.float32).astype(ml_dtypes.float8_e4m3fn).view(np.uint8)
    words = codes.reshape(n // 512, 128, 4, m).transpose(0, 1, 3, 2)
    return np.ascontiguousarray(words), np.ascontiguousarray(byte.astype(np.uint8).reshape(n // 512, 16, m))


K, T, S, H, C = 512, 2048, 512, 512, 512


def setup_inputs():
    n = np.random.standard_normal
    s = mx_kscale(K)[:, None]
    packed_xT = pack_weight(n((K, T)) * s)
    packed_w1 = pack_weight(n((K, H)) / np.sqrt(K) / s)
    return {
        "x_words": packed_xT[0],
        "x_scales": packed_xT[1],
        "w1_words": packed_w1[0],
        "w1_scales": packed_w1[1],
        "gs": (np.random.uniform(0.5, 1.5, (K, 1)) / s).astype(np.float32),
        "offs": striped(np.random.permutation(T)[:S]),
        "n1": striped8(np.stack([np.random.permutation(S) for _ in range(8)])),
        "n2": striped8(np.stack([np.random.permutation(S) for _ in range(8)])),
        "ca": striped(np.random.permutation(T)[:C]),
        "cb": striped(np.random.permutation(T)[:C]),
        "cd": striped(np.random.permutation(T)[:C]),
        "n3": striped8(np.stack([np.random.permutation(S) for _ in range(8)])),
        "n4": striped8(np.stack([np.random.permutation(S) for _ in range(8)])),
        "n5": striped8(np.stack([np.random.permutation(S) for _ in range(8)])),
        "n6": striped8(np.stack([np.random.permutation(S) for _ in range(8)])),
        "n7": striped8(np.stack([np.random.permutation(S) for _ in range(8)])),
    }


def reference(x_words, x_scales, w1_words, w1_scales, gs, offs, n1, n2, ca, cb, cd, n3, n4, n5, n6, n7):
    x_cb = unpack_weight(x_words, x_scales)[:, unstriped(cb)]
    xq = unpack_weight(x_words, x_scales)[:, unstriped(offs)]
    y = unpack_weight(w1_words, w1_scales).T @ xq
    pa = y[np.arange(H)[:, None], runs(n1, H)]
    pb = y[np.arange(H)[:, None], runs(n2, H)]
    z = f64(gs) * (np.maximum(np.minimum(y, pa), np.minimum(np.maximum(y, pa), pb)))
    zq = mxq(z, 0, "e4m3")
    b = 0.0625 * (x_cb.T @ zq)
    x_ca = unpack_weight(x_words, x_scales)[:, unstriped(ca)]
    a = 0.0625 * (x_ca.T @ zq)
    m1 = b * (a[np.arange(C)[:, None], runs(n3, C)] - a) + 0.5 * ((b[np.arange(C)[:, None], runs(n5, C)]) * (a[np.arange(C)[:, None], runs(n4, C)] - a))
    x_cd = unpack_weight(x_words, x_scales)[:, unstriped(cd)]
    q = 0.0625 * (x_cd.T @ zq)
    out_0 = np.maximum(m1, q[np.arange(C)[:, None], runs(n7, C)]) - (np.minimum(m1[np.arange(C)[:, None], runs(n6, C)], q))
    return (out_0,) + planes(out_0)

@@ -1,0 +1,259 @@
+from contextlib import ExitStack
+
+import concourse.mybir as mybir
+
+F32 = mybir.dt.float32
+BF16 = mybir.dt.bfloat16
+I32 = mybir.dt.int32
+U32 = mybir.dt.uint32
+U16 = mybir.dt.uint16
+U8 = mybir.dt.uint8
+FP8X4 = mybir.dt.float8_e4m3fn_x4
+ALU = mybir.AluOpType
+COPY = mybir.ActivationFunctionType.Copy
+
+P = 128
+T = 2048
+S = 512
+PACK = 4
+HALF = S // 2
+SIXTEENTH = 0.0625
+FLOPS = 4 * 2 * 512 * 512 * 512
+FUSED_TILES = 3
+PIECES = ((0, 256), (256, 128), (384, 128))
+
+
+def tile_picked_tricdflowbmaxbmed_none_po_kernel(
+    tc, x_words, x_scales, w1_words, w1_scales, gs, offs, n1, n2, ca, cb, cd, n3, n4, n5, n6, n7, out_0, out_1, out_2
+):
+    nc = tc.nc
+    with ExitStack() as ctx:
+        keep = ctx.enter_context(tc.tile_pool(name="keep", bufs=1))
+        psum = ctx.enter_context(tc.psum_pool(name="psum", bufs=1))
+
+        def sbuf(name, shape, dtype, tag=None):
+            return keep.tile(shape, dtype, name=name, tag=tag or name, align_bytes=64)
+
+        def bank(number, name):
+            return psum.tile([P, S], F32, name=name, tag="bank%d" % number)
+
+        def load_list(name, source):
+            tile = sbuf("list_" + name, [P, S // 16], U16)
+            nc.sync.dma_start(tile[:], source)
+            return tile
+
+        def load_scale_rows(tile, source):
+            for quadrant in range(4):
+                nc.sync.dma_start(
+                    tile[32 * quadrant : 32 * quadrant + 4, :].bitcast(I32),
+                    source[0, 4 * quadrant : 4 * quadrant + 4, :].bitcast(I32),
+                )
+
+        def entries(lst, start, count):
+            return lst[:, start // 16 : (start + count) // 16]
+
+        def dealt(ap):
+            return ap.rearrange("p (t m) -> p m t", t=PACK)
+
+        xs = sbuf("xs", [P, T], U8)
+        ws = sbuf("ws", [P, S], U8)
+        nc.vector.memset(xs[:].bitcast(I32), 0)
+        nc.vector.memset(ws[:].bitcast(I32), 0)
+        ww = sbuf("ww", [P, S], I32)
+        nc.sync.dma_start(ww[:], w1_words[0].rearrange("p c r -> p (c r)").bitcast(I32))
+        load_scale_rows(xs, x_scales)
+        l_offs = load_list("offs", offs)
+        l_ca = load_list("ca", ca)
+        xw = sbuf("xw", [P, T], I32)
+        nc.sync.dma_start(xw[:], x_words[0].rearrange("p c r -> p (c r)").bitcast(I32))
+        load_scale_rows(ws, w1_scales)
+        gain = sbuf("gain", [P, PACK], F32)
+        nc.sync.dma_start(gain[:], gs.rearrange("(p t) o -> p (t o)", t=PACK))
+        l_n1 = load_list("n1", n1)
+        l_n2 = load_list("n2", n2)
+        l_cb = load_list("cb", cb)
+        l_cd = load_list("cd", cd)
+        l_n4 = load_list("n4", n4)
+        l_n3 = load_list("n3", n3)
+        l_n5 = load_list("n5", n5)
+        l_n7 = load_list("n7", n7)
+        l_n6 = load_list("n6", n6)
+
+        def pick_bytes(name, lst, tag=None):
+            picked = sbuf(name + "_bytes", [P, S], U8, tag)
+            nc.vector.tensor_copy(picked[:], xs[:].indirect(lst[:]))
+            return picked
+
+        def deal_bytes(name, source):
+            result = sbuf(name + "_dealt_bytes", [P, S], U8)
+            nc.vector.tensor_copy(
+                result[:].rearrange("p (t m) -> p t m", t=PACK), source[:].rearrange("p (m t) -> p t m", t=PACK)
+            )
+            return result
+
+        def pick_dealt_words(name, lst, tag=None):
+            picked = sbuf(name + "_words", [P, S], U32, tag)
+            nc.vector.tensor_copy(dealt(picked[:]), xw[:].bitcast(U32).indirect(lst[:]))
+            return picked
+
+        def product(out, words, scales, t, moving_words, moving_scales):
+            cols = slice(P * t, P * (t + 1))
+            nc.tensor.matmul_mx(
+                out=out,
+                lhsT=words[:, cols].bitcast(FP8X4),
+                lhsT_scale=scales[:, cols],
+                rhs=moving_words.bitcast(FP8X4),
+                rhs_scale=moving_scales,
+                start=True,
+                stop=True,
+            )
+
+        xq_bytes = pick_bytes("xq", l_offs)
+        xq_words = sbuf("xq_words", [P, S], U32)
+        nc.vector.tensor_copy(xq_words[:], xw[:].bitcast(U32).indirect(l_offs[:]))
+        w_words = sbuf("w_words", [P, S], I32)
+        nc.vector.tensor_copy(dealt(w_words[:]), ww[:].rearrange("p (m t) -> p m t", t=PACK))
+        w_scales = deal_bytes("w", ws)
+
+        y = [sbuf("y%d" % t, [P, S], F32) for t in range(PACK)]
+        y_banks = []
+        for t in range(PACK):
+            y_banks.append(bank(t, "y_bank%d" % t))
+            product(y_banks[t][:], w_words, w_scales, t, xq_words[:], xq_bytes[:])
+
+        ca_scales = deal_bytes("ca", pick_bytes("ca", l_ca))
+        ca_words = pick_dealt_words("ca", l_ca)
+        cb_scales = deal_bytes("cb", pick_bytes("cb", l_cb))
+        cb_words = pick_dealt_words("cb", l_cb)
+
+        z_words = sbuf("z_words", [P, S], U32)
+        z_scales = sbuf("z_scales", [P, S], U8)
+        a = [sbuf("a%d" % t, [P, S], F32) for t in range(PACK)]
+        b = [sbuf("b%d" % t, [P, S], F32) for t in range(PACK)]
+        ab_banks = {}
+        for h in range(2):
+            cols = slice(HALF * h, HALF * (h + 1))
+            pa = sbuf("pa%d" % h, [P, PACK, HALF], F32)
+            pb = sbuf("pb%d" % h, [P, PACK, HALF], F32)
+            low = sbuf("low%d" % h, [P, PACK, HALF], F32)
+            high = sbuf("high%d" % h, [P, PACK, HALF], F32)
+            capped = sbuf("capped%d" % h, [P, PACK, HALF], F32)
+            for t in range(PACK):
+                if h == 0:
+                    nc.scalar.activation(y[t][:], y_banks[t][:], COPY, scale=gain[:, t : t + 1])
+                nc.scalar.activation(pa[:, t, :], y[t][:].indirect(entries(l_n1, HALF * h, HALF)), COPY)
+                nc.scalar.activation(pb[:, t, :], y[t][:].indirect(entries(l_n2, HALF * h, HALF)), COPY)
+                nc.vector.tensor_tensor(high[:, t, :], y[t][:, cols], pa[:, t, :], ALU.max)
+                nc.vector.tensor_tensor(low[:, t, :], y[t][:, cols], pa[:, t, :], ALU.min)
+                nc.vector.tensor_tensor(capped[:, t, :], high[:, t, :], pb[:, t, :], ALU.min)
+            z = sbuf("z%d" % h, [P, HALF, PACK], BF16)
+            nc.vector.tensor_tensor(
+                z[:].rearrange("p (c i) t -> p c t i", i=4),
+                low[:].rearrange("p t (c i) -> p c t i", i=4),
+                capped[:].rearrange("p t (c i) -> p c t i", i=4),
+                ALU.max,
+            )
+            nc.vector.quantize_mx(
+                out=z_words[:, cols].bitcast(FP8X4), scales=z_scales[:, cols], in_=z[:].rearrange("p s t -> p (s t)")
+            )
+            for t in range(PACK):
+                both = bank(4 * (1 - h) + t, "ab_bank%d_%d" % (h, t))
+                ab_banks[(h, t)] = both
+                product(both[:, 0:HALF], ca_words, ca_scales, t, z_words[:, cols], z_scales[:, cols])
+                product(both[:, HALF:S], cb_words, cb_scales, t, z_words[:, cols], z_scales[:, cols])
+                if h == 0:
+                    nc.scalar.activation(a[t][:, cols], both[:, 0:HALF], COPY, scale=SIXTEENTH)
+                    nc.scalar.activation(b[t][:, cols], both[:, HALF:S], COPY, scale=SIXTEENTH)
+
+        cd_scales = deal_bytes("cd", pick_bytes("cd", l_cd, "capped1"))
+        cd_words = pick_dealt_words("cd", l_cd, "low1")
+
+        m1 = [sbuf("m1_%d" % t, [P, S], F32) for t in range(PACK)]
+        q = [sbuf("q%d" % t, [P, S], F32) for t in range(PACK)]
+        result = sbuf("result", [P, PACK, S], F32)
+        out_rows = out_0.rearrange("(p t) s -> p t s", t=PACK)
+
+        def fetch(name, window, lst):
+            fetched = sbuf(name, [P, S], F32)
+            for h in range(2):
+                nc.scalar.activation(
+                    fetched[:, HALF * h : HALF * (h + 1)], window[:].indirect(entries(lst, HALF * h, HALF)), COPY
+                )
+            return fetched
+
+        def flow(t):
+            both = ab_banks[(1, t)]
+            nc.scalar.activation(a[t][:, HALF:S], both[:, 0:HALF], COPY, scale=SIXTEENTH)
+            nc.scalar.activation(b[t][:, HALF:S], both[:, HALF:S], COPY, scale=SIXTEENTH)
+            a4 = fetch("a4_%d" % t, a[t], l_n4)
+            a3 = fetch("a3_%d" % t, a[t], l_n3)
+            d4 = sbuf("d4_%d" % t, [P, S], F32)
+            d3 = sbuf("d3_%d" % t, [P, S], F32)
+            second = sbuf("second%d" % t, [P, S], F32)
+            first = sbuf("first%d" % t, [P, S], F32)
+            nc.vector.tensor_tensor(d4[:], a4[:], a[t][:], ALU.subtract)
+            nc.vector.tensor_tensor(d3[:], a3[:], a[t][:], ALU.subtract)
+            if t < FUSED_TILES:
+                for h in range(2):
+                    cols = slice(HALF * h, HALF * (h + 1))
+                    nc.vector.tensor_tensor(
+                        second[:, cols], b[t][:].indirect(entries(l_n5, HALF * h, HALF)), d4[:, cols], ALU.mult
+                    )
+            else:
+                b5 = fetch("b5_%d" % t, b[t], l_n5)
+                nc.vector.tensor_tensor(second[:], b5[:], d4[:], ALU.mult)
+            nc.vector.tensor_tensor(first[:], b[t][:], d3[:], ALU.mult)
+            nc.vector.scalar_tensor_tensor(m1[t][:], second[:], 0.5, first[:], ALU.mult, ALU.add)
+
+        def score(t):
+            q_bank = bank(4 + t, "q_bank%d" % t)
+            product(q_bank[:], cd_words, cd_scales, t, z_words[:], z_scales[:])
+            nc.scalar.activation(q[t][:], q_bank[:], COPY, scale=SIXTEENTH)
+            return fetch("q7_%d" % t, q[t], l_n7)
+
+        def combine(t, q7, start, count):
+            cols = slice(start, start + count)
+            m6 = sbuf("m6_%d_%d" % (t, start), [P, count], F32)
+            for piece in range(0, count, HALF):
+                width = min(HALF, count - piece)
+                nc.scalar.activation(
+                    m6[:, piece : piece + width], m1[t][:].indirect(entries(l_n6, start + piece, width)), COPY
+                )
+            larger = sbuf("larger%d_%d" % (t, start), [P, count], F32)
+            smaller = sbuf("smaller%d_%d" % (t, start), [P, count], F32)
+            nc.vector.tensor_tensor(larger[:], m1[t][:, cols], q7[:, cols], ALU.max)
+            nc.vector.tensor_tensor(smaller[:], m6[:], q[t][:, cols], ALU.min)
+            nc.vector.tensor_tensor(result[:, t, cols], larger[:], smaller[:], ALU.subtract)
+            nc.sync.dma_start(out_rows[:, t, cols], result[:, t, cols])
+
+        flow(0)
+        for t in range(PACK - 1):
+            flow(t + 1)
+            combine(t, score(t), 0, S)
+
+        last = PACK - 1
+        q7_last = score(last)
+        out_words = sbuf("out_words", [P, S], U32)
+        out_scales = sbuf("out_scales", [P, S], U8)
+        words_hbm = out_1[0].rearrange("p c r -> p (c r)").bitcast(I32)
+        for number, (start, count) in enumerate(PIECES):
+            cols = slice(start, start + count)
+            combine(last, q7_last, start, count)
+            rounded = sbuf("rounded%d" % start, [P, count, PACK], BF16)
+            target = rounded[:].rearrange("p (c i) t -> p c t i", i=4)
+            source = result[:, :, cols].rearrange("p t (c i) -> p c t i", i=4)
+            if number == 0:
+                nc.scalar.copy(target, source)
+            else:
+                nc.vector.tensor_copy(target, source)
+            nc.vector.quantize_mx(
+                out=out_words[:, cols].bitcast(FP8X4),
+                scales=out_scales[:, cols],
+                in_=rounded[:].rearrange("p s t -> p (s t)"),
+            )
+            nc.sync.dma_start(words_hbm[:, cols], out_words[:, cols].bitcast(I32))
+        for quadrant in range(4):
+            nc.scalar.dma_start(
+                out_2[0, 4 * quadrant : 4 * quadrant + 4, :].bitcast(I32),
+                out_scales[32 * quadrant : 32 * quadrant + 4, :].bitcast(I32),
+            )

@@ -19,8 +19,6 @@ PACK = 4
 HALF = S // 2
 SIXTEENTH = 0.0625
 FLOPS = 4 * 2 * 512 * 512 * 512
-FUSED_TILES = 3
-PIECES = ((0, 256), (256, 128), (384, 128))
 
 
 def tile_picked_tricdflowbmaxbmed_none_po_kernel(
@@ -45,8 +43,8 @@ def tile_picked_tricdflowbmaxbmed_none_po_kernel(
         def load_scale_rows(tile, source):
             for quadrant in range(4):
                 nc.sync.dma_start(
-                    tile[32 * quadrant : 32 * quadrant + 4, :].bitcast(I32),
-                    source[0, 4 * quadrant : 4 * quadrant + 4, :].bitcast(I32),
+                    tile[32 * quadrant : 32 * (quadrant + 1), :].bitcast(I32),
+                    source[0, 4 * quadrant : 4 * quadrant + 4, :].bitcast(I32).partition_broadcast(8),
                 )
 
         def entries(lst, start, count):
@@ -57,13 +55,11 @@ def tile_picked_tricdflowbmaxbmed_none_po_kernel(
 
         xs = sbuf("xs", [P, T], U8)
         ws = sbuf("ws", [P, S], U8)
-        nc.vector.memset(xs[:].bitcast(I32), 0)
-        nc.vector.memset(ws[:].bitcast(I32), 0)
-        ww = sbuf("ww", [P, S], I32)
-        nc.sync.dma_start(ww[:], w1_words[0].rearrange("p c r -> p (c r)").bitcast(I32))
         load_scale_rows(xs, x_scales)
         l_offs = load_list("offs", offs)
         l_ca = load_list("ca", ca)
+        ww = sbuf("ww", [P, S], I32)
+        nc.sync.dma_start(ww[:], w1_words[0].rearrange("p c r -> p (c r)").bitcast(I32))
         xw = sbuf("xw", [P, T], I32)
         nc.sync.dma_start(xw[:], x_words[0].rearrange("p c r -> p (c r)").bitcast(I32))
         load_scale_rows(ws, w1_scales)
@@ -84,8 +80,8 @@ def tile_picked_tricdflowbmaxbmed_none_po_kernel(
             nc.vector.tensor_copy(picked[:], xs[:].indirect(lst[:]))
             return picked
 
-        def deal_bytes(name, source):
-            result = sbuf(name + "_dealt_bytes", [P, S], U8)
+        def deal_bytes(name, source, tag=None):
+            result = sbuf(name + "_dealt_bytes", [P, S], U8, tag)
             nc.vector.tensor_copy(
                 result[:].rearrange("p (t m) -> p t m", t=PACK), source[:].rearrange("p (m t) -> p t m", t=PACK)
             )
@@ -121,35 +117,44 @@ def tile_picked_tricdflowbmaxbmed_none_po_kernel(
             y_banks.append(bank(t, "y_bank%d" % t))
             product(y_banks[t][:], w_words, w_scales, t, xq_words[:], xq_bytes[:])
 
-        ca_scales = deal_bytes("ca", pick_bytes("ca", l_ca))
-        ca_words = pick_dealt_words("ca", l_ca)
-        cb_scales = deal_bytes("cb", pick_bytes("cb", l_cb))
+        ca_scales = deal_bytes("ca", pick_bytes("ca", l_ca), "ws")
+        ca_words = pick_dealt_words("ca", l_ca, "ca_bytes")
+        cb_bytes = pick_bytes("cb", l_cb)
         cb_words = pick_dealt_words("cb", l_cb)
+        cb_scales = deal_bytes("cb", cb_bytes)
 
         z_words = sbuf("z_words", [P, S], U32)
         z_scales = sbuf("z_scales", [P, S], U8)
-        a = [sbuf("a%d" % t, [P, S], F32) for t in range(PACK)]
-        b = [sbuf("b%d" % t, [P, S], F32) for t in range(PACK)]
+        a_win = [sbuf("a%d" % t, [P, 2 * S], F32) for t in range(PACK)]
+        b_win = [sbuf("b%d" % t, [P, 3 * S if t else S], F32) for t in range(PACK)]
+        q_win = [sbuf("q%d" % t, [P, 3 * S], F32) for t in range(PACK)]
+        m_win = [sbuf("m%d" % t, [P, 2 * S], F32) for t in range(PACK)]
+        low = sbuf("low", [P, PACK, S], F32)
+        high = sbuf("high", [P, PACK, S], F32)
+        pb = [sbuf("pb%d" % h, [P, PACK, HALF], F32) for h in range(2)]
+        for t in range(PACK):
+            pa = a_win[t][:, S : 2 * S]
+            nc.scalar.activation(y[t][:], y_banks[t][:], COPY, scale=gain[:, t : t + 1])
+            for h in range(2):
+                nc.scalar.activation(
+                    pa[:, HALF * h : HALF * (h + 1)], y[t][:].indirect(entries(l_n1, HALF * h, HALF)), COPY
+                )
+            nc.vector.tensor_tensor(high[:, t, :], y[t][:], pa, ALU.max)
+            nc.vector.tensor_tensor(low[:, t, :], y[t][:], pa, ALU.min)
+        for h in range(2):
+            for t in range(PACK):
+                nc.scalar.activation(pb[h][:, t, :], y[t][:].indirect(entries(l_n2, HALF * h, HALF)), COPY)
         ab_banks = {}
+        a_plain = sbuf("a_plain", [P, S], F32)
         for h in range(2):
             cols = slice(HALF * h, HALF * (h + 1))
-            pa = sbuf("pa%d" % h, [P, PACK, HALF], F32)
-            pb = sbuf("pb%d" % h, [P, PACK, HALF], F32)
-            low = sbuf("low%d" % h, [P, PACK, HALF], F32)
-            high = sbuf("high%d" % h, [P, PACK, HALF], F32)
-            capped = sbuf("capped%d" % h, [P, PACK, HALF], F32)
-            for t in range(PACK):
-                if h == 0:
-                    nc.scalar.activation(y[t][:], y_banks[t][:], COPY, scale=gain[:, t : t + 1])
-                nc.scalar.activation(pa[:, t, :], y[t][:].indirect(entries(l_n1, HALF * h, HALF)), COPY)
-                nc.scalar.activation(pb[:, t, :], y[t][:].indirect(entries(l_n2, HALF * h, HALF)), COPY)
-                nc.vector.tensor_tensor(high[:, t, :], y[t][:, cols], pa[:, t, :], ALU.max)
-                nc.vector.tensor_tensor(low[:, t, :], y[t][:, cols], pa[:, t, :], ALU.min)
-                nc.vector.tensor_tensor(capped[:, t, :], high[:, t, :], pb[:, t, :], ALU.min)
+            capped = sbuf("capped%d" % h, [P, PACK, HALF], F32, "capped")
+            for tiles in (slice(0, PACK - 1), slice(PACK - 1, PACK)):
+                nc.vector.tensor_tensor(capped[:, tiles, :], high[:, tiles, cols], pb[h][:, tiles, :], ALU.min)
             z = sbuf("z%d" % h, [P, HALF, PACK], BF16)
             nc.vector.tensor_tensor(
                 z[:].rearrange("p (c i) t -> p c t i", i=4),
-                low[:].rearrange("p t (c i) -> p c t i", i=4),
+                low[:, :, cols].rearrange("p t (c i) -> p c t i", i=4),
                 capped[:].rearrange("p t (c i) -> p c t i", i=4),
                 ALU.max,
             )
@@ -162,94 +167,128 @@ def tile_picked_tricdflowbmaxbmed_none_po_kernel(
                 product(both[:, 0:HALF], ca_words, ca_scales, t, z_words[:, cols], z_scales[:, cols])
                 product(both[:, HALF:S], cb_words, cb_scales, t, z_words[:, cols], z_scales[:, cols])
                 if h == 0:
-                    nc.scalar.activation(a[t][:, cols], both[:, 0:HALF], COPY, scale=SIXTEENTH)
-                    nc.scalar.activation(b[t][:, cols], both[:, HALF:S], COPY, scale=SIXTEENTH)
+                    nc.scalar.activation(a_win[t][:, cols], both[:, 0:HALF], COPY, scale=SIXTEENTH)
+                    if t == 0:
+                        nc.scalar.activation(a_plain[:, cols], both[:, 0:HALF], COPY, scale=SIXTEENTH)
+                    nc.scalar.activation(b_win[t][:, cols], both[:, HALF:S], COPY, scale=SIXTEENTH)
 
-        cd_scales = deal_bytes("cd", pick_bytes("cd", l_cd, "capped1"))
-        cd_words = pick_dealt_words("cd", l_cd, "low1")
+        cd_bytes = pick_bytes("cd", l_cd, "capped")
+        cd_words = pick_dealt_words("cd", l_cd, "low")
+        cd_scales = deal_bytes("cd", cd_bytes)
 
-        m1 = [sbuf("m1_%d" % t, [P, S], F32) for t in range(PACK)]
-        q = [sbuf("q%d" % t, [P, S], F32) for t in range(PACK)]
         result = sbuf("result", [P, PACK, S], F32)
         out_rows = out_0.rearrange("(p t) s -> p t s", t=PACK)
 
-        def fetch(name, window, lst):
-            fetched = sbuf(name, [P, S], F32)
-            for h in range(2):
-                nc.scalar.activation(
-                    fetched[:, HALF * h : HALF * (h + 1)], window[:].indirect(entries(lst, HALF * h, HALF)), COPY
-                )
-            return fetched
+        second = [sbuf("second%d" % t, [P, S], F32) for t in range(PACK)]
+        q7 = [sbuf("q7_%d" % t, [P, S], F32) for t in range(PACK)]
+        m6 = [sbuf("m6_%d" % t, [P, S], F32) for t in range(PACK)]
+        larger = [sbuf("larger%d" % t, [P, S], F32) for t in range(PACK)]
+        smaller = [sbuf("smaller%d" % t, [P, S], F32) for t in range(PACK)]
+        whole = slice(0, S)
 
-        def flow(t):
+        def differences(t):
             both = ab_banks[(1, t)]
-            nc.scalar.activation(a[t][:, HALF:S], both[:, 0:HALF], COPY, scale=SIXTEENTH)
-            nc.scalar.activation(b[t][:, HALF:S], both[:, HALF:S], COPY, scale=SIXTEENTH)
-            a4 = fetch("a4_%d" % t, a[t], l_n4)
-            a3 = fetch("a3_%d" % t, a[t], l_n3)
-            d4 = sbuf("d4_%d" % t, [P, S], F32)
-            d3 = sbuf("d3_%d" % t, [P, S], F32)
-            second = sbuf("second%d" % t, [P, S], F32)
-            first = sbuf("first%d" % t, [P, S], F32)
-            nc.vector.tensor_tensor(d4[:], a4[:], a[t][:], ALU.subtract)
-            nc.vector.tensor_tensor(d3[:], a3[:], a[t][:], ALU.subtract)
-            if t < FUSED_TILES:
-                for h in range(2):
-                    cols = slice(HALF * h, HALF * (h + 1))
-                    nc.vector.tensor_tensor(
-                        second[:, cols], b[t][:].indirect(entries(l_n5, HALF * h, HALF)), d4[:, cols], ALU.mult
-                    )
+            nc.scalar.activation(a_win[t][:, HALF:S], both[:, 0:HALF], COPY, scale=SIXTEENTH)
+            if t == 0:
+                nc.scalar.activation(a_plain[:, HALF:S], both[:, 0:HALF], COPY, scale=SIXTEENTH)
+                nc.scalar.activation(b_win[t][:, HALF:S], both[:, HALF:S], COPY, scale=SIXTEENTH)
+                nc.vector.tensor_tensor(
+                    q_win[t][:, 2 * S : 3 * S], a_win[t][:].indirect(l_n3[:]), a_plain[:], ALU.subtract
+                )
+                nc.vector.tensor_tensor(q_win[t][:, S : 2 * S], a_win[t][:].indirect(l_n4[:]), a_plain[:], ALU.subtract)
             else:
-                b5 = fetch("b5_%d" % t, b[t], l_n5)
-                nc.vector.tensor_tensor(second[:], b5[:], d4[:], ALU.mult)
-            nc.vector.tensor_tensor(first[:], b[t][:], d3[:], ALU.mult)
-            nc.vector.scalar_tensor_tensor(m1[t][:], second[:], 0.5, first[:], ALU.mult, ALU.add)
+                nc.scalar.activation(b_win[t][:, S : 2 * S], a_win[t][:].indirect(l_n4[:]), COPY)
+                nc.scalar.activation(b_win[t][:, 2 * S : 3 * S], a_win[t][:].indirect(l_n3[:]), COPY)
+                nc.scalar.activation(b_win[t][:, HALF:S], both[:, HALF:S], COPY, scale=SIXTEENTH)
+                nc.vector.tensor_tensor(
+                    q_win[t][:, S : 3 * S].rearrange("p (k s) -> p k s", k=2),
+                    b_win[t][:, S : 3 * S].rearrange("p (k s) -> p k s", k=2),
+                    a_win[t][:, 0:S].unsqueeze(1).to_broadcast([P, 2, S]),
+                    ALU.subtract,
+                )
+
+        def terms(t):
+            nc.vector.tensor_tensor(m_win[t][:, S : 2 * S], b_win[t][:, 0:S], q_win[t][:, 2 * S : 3 * S], ALU.mult)
+            width = S if t else HALF
+            for start in range(0, S, width):
+                nc.vector.tensor_tensor(
+                    second[t][:, start : start + width],
+                    b_win[t][:].indirect(entries(l_n5, start, width)),
+                    q_win[t][:, S + start : S + start + width],
+                    ALU.mult,
+                )
+
+        def join_terms(t):
+            nc.vector.scalar_tensor_tensor(
+                m_win[t][:, 0:S], second[t][:], 0.5, m_win[t][:, S : 2 * S], ALU.mult, ALU.add
+            )
 
         def score(t):
             q_bank = bank(4 + t, "q_bank%d" % t)
             product(q_bank[:], cd_words, cd_scales, t, z_words[:], z_scales[:])
-            nc.scalar.activation(q[t][:], q_bank[:], COPY, scale=SIXTEENTH)
-            return fetch("q7_%d" % t, q[t], l_n7)
+            nc.scalar.activation(q_win[t][:, 0:S], q_bank[:], COPY, scale=SIXTEENTH)
+            nc.scalar.activation(q7[t][:], q_win[t][:].indirect(l_n7[:]), COPY)
 
-        def combine(t, q7, start, count):
-            cols = slice(start, start + count)
-            m6 = sbuf("m6_%d_%d" % (t, start), [P, count], F32)
-            for piece in range(0, count, HALF):
-                width = min(HALF, count - piece)
-                nc.scalar.activation(
-                    m6[:, piece : piece + width], m1[t][:].indirect(entries(l_n6, start + piece, width)), COPY
-                )
-            larger = sbuf("larger%d_%d" % (t, start), [P, count], F32)
-            smaller = sbuf("smaller%d_%d" % (t, start), [P, count], F32)
-            nc.vector.tensor_tensor(larger[:], m1[t][:, cols], q7[:, cols], ALU.max)
-            nc.vector.tensor_tensor(smaller[:], m6[:], q[t][:, cols], ALU.min)
-            nc.vector.tensor_tensor(result[:, t, cols], larger[:], smaller[:], ALU.subtract)
+        def fetch_m6(t, cols):
+            nc.scalar.activation(
+                m6[t][:, cols], m_win[t][:].indirect(entries(l_n6, cols.start, cols.stop - cols.start)), COPY
+            )
+
+        def take_larger(t):
+            nc.vector.tensor_tensor(larger[t][:], m_win[t][:, 0:S], q7[t][:], ALU.max)
+
+        def take_smaller(t, cols):
+            nc.vector.tensor_tensor(smaller[t][:, cols], m6[t][:, cols], q_win[t][:, cols], ALU.min)
+
+        def finish(t, cols):
+            nc.vector.tensor_tensor(result[:, t, cols], larger[t][:, cols], smaller[t][:, cols], ALU.subtract)
             nc.sync.dma_start(out_rows[:, t, cols], result[:, t, cols])
 
-        flow(0)
-        for t in range(PACK - 1):
-            flow(t + 1)
-            combine(t, score(t), 0, S)
+        for t in range(PACK):
+            done = t - 2
+            differences(t)
+            if done >= 0:
+                fetch_m6(done, whole)
+                take_larger(done)
+            terms(t)
+            if done >= 0:
+                take_smaller(done, whole)
+            join_terms(t)
+            if done >= 0:
+                finish(done, whole)
+            if t >= 1:
+                score(t - 1)
 
         last = PACK - 1
-        q7_last = score(last)
+        halves = (slice(0, HALF), slice(HALF, S))
+        fetch_m6(last - 1, whole)
+        score(last)
+        take_larger(last - 1)
+        take_smaller(last - 1, whole)
+        take_larger(last)
+        finish(last - 1, whole)
+        for cols in halves:
+            fetch_m6(last, cols)
+            take_smaller(last, cols)
+        for cols in halves:
+            finish(last, cols)
+
         out_words = sbuf("out_words", [P, S], U32)
         out_scales = sbuf("out_scales", [P, S], U8)
         words_hbm = out_1[0].rearrange("p c r -> p (c r)").bitcast(I32)
-        for number, (start, count) in enumerate(PIECES):
-            cols = slice(start, start + count)
-            combine(last, q7_last, start, count)
-            rounded = sbuf("rounded%d" % start, [P, count, PACK], BF16)
-            target = rounded[:].rearrange("p (c i) t -> p c t i", i=4)
+        rounded = [sbuf("rounded%d" % h, [P, HALF, PACK], BF16) for h in range(2)]
+        for h, cols in enumerate(halves):
+            target = rounded[h][:].rearrange("p (c i) t -> p c t i", i=4)
             source = result[:, :, cols].rearrange("p t (c i) -> p c t i", i=4)
-            if number == 0:
+            if h == 0:
                 nc.scalar.copy(target, source)
             else:
                 nc.vector.tensor_copy(target, source)
+        for h, cols in enumerate(halves):
             nc.vector.quantize_mx(
                 out=out_words[:, cols].bitcast(FP8X4),
                 scales=out_scales[:, cols],
-                in_=rounded[:].rearrange("p s t -> p (s t)"),
+                in_=rounded[h][:].rearrange("p s t -> p (s t)"),
             )
             nc.sync.dma_start(words_hbm[:, cols], out_words[:, cols].bitcast(I32))
         for quadrant in range(4):

@@ -58,16 +58,16 @@ def tile_picked_tricdflowbmaxbmed_none_po_kernel(
         load_scale_rows(xs, x_scales)
         l_offs = load_list("offs", offs)
         l_ca = load_list("ca", ca)
-        ww = sbuf("ww", [P, S], I32)
-        nc.sync.dma_start(ww[:], w1_words[0].rearrange("p c r -> p (c r)").bitcast(I32))
         xw = sbuf("xw", [P, T], I32)
         nc.sync.dma_start(xw[:], x_words[0].rearrange("p c r -> p (c r)").bitcast(I32))
+        ww = sbuf("ww", [P, S], I32)
+        nc.sync.dma_start(ww[:], w1_words[0].rearrange("p c r -> p (c r)").bitcast(I32))
         load_scale_rows(ws, w1_scales)
         gain = sbuf("gain", [P, PACK], F32)
         nc.sync.dma_start(gain[:], gs.rearrange("(p t) o -> p (t o)", t=PACK))
+        l_cb = load_list("cb", cb)
         l_n1 = load_list("n1", n1)
         l_n2 = load_list("n2", n2)
-        l_cb = load_list("cb", cb)
         l_cd = load_list("cd", cd)
         l_n4 = load_list("n4", n4)
         l_n3 = load_list("n3", n3)
@@ -153,9 +153,9 @@ def tile_picked_tricdflowbmaxbmed_none_po_kernel(
                 nc.vector.tensor_tensor(capped[:, tiles, :], high[:, tiles, cols], pb[h][:, tiles, :], ALU.min)
             z = sbuf("z%d" % h, [P, HALF, PACK], BF16)
             nc.vector.tensor_tensor(
-                z[:].rearrange("p (c i) t -> p c t i", i=4),
-                low[:, :, cols].rearrange("p t (c i) -> p c t i", i=4),
-                capped[:].rearrange("p t (c i) -> p c t i", i=4),
+                z[:].rearrange("p (c i) t -> p c t i", i=2),
+                low[:, :, cols].rearrange("p t (c i) -> p c t i", i=2),
+                capped[:].rearrange("p t (c i) -> p c t i", i=2),
                 ALU.max,
             )
             nc.vector.quantize_mx(
@@ -264,22 +264,21 @@ def tile_picked_tricdflowbmaxbmed_none_po_kernel(
         fetch_m6(last - 1, whole)
         score(last)
         take_larger(last - 1)
-        take_smaller(last - 1, whole)
         take_larger(last)
-        finish(last - 1, whole)
         for cols in halves:
             fetch_m6(last, cols)
-            take_smaller(last, cols)
-        for cols in halves:
-            finish(last, cols)
+            for t in (last - 1, last):
+                take_smaller(t, cols)
+            for t in (last - 1, last):
+                finish(t, cols)
 
         out_words = sbuf("out_words", [P, S], U32)
         out_scales = sbuf("out_scales", [P, S], U8)
         words_hbm = out_1[0].rearrange("p c r -> p (c r)").bitcast(I32)
         rounded = [sbuf("rounded%d" % h, [P, HALF, PACK], BF16) for h in range(2)]
         for h, cols in enumerate(halves):
-            target = rounded[h][:].rearrange("p (c i) t -> p c t i", i=4)
-            source = result[:, :, cols].rearrange("p t (c i) -> p c t i", i=4)
+            target = rounded[h][:].rearrange("p (c i) t -> p c t i", i=2)
+            source = result[:, :, cols].rearrange("p t (c i) -> p c t i", i=2)
             if h == 0:
                 nc.scalar.copy(target, source)
             else:
@@ -292,7 +291,7 @@ def tile_picked_tricdflowbmaxbmed_none_po_kernel(
             )
             nc.sync.dma_start(words_hbm[:, cols], out_words[:, cols].bitcast(I32))
         for quadrant in range(4):
-            nc.scalar.dma_start(
+            (nc.scalar if quadrant % 2 else nc.sync).dma_start(
                 out_2[0, 4 * quadrant : 4 * quadrant + 4, :].bitcast(I32),
                 out_scales[32 * quadrant : 32 * quadrant + 4, :].bitcast(I32),
             )

from contextlib import ExitStack

import concourse.mybir as mybir

F32 = mybir.dt.float32
BF16 = mybir.dt.bfloat16
I32 = mybir.dt.int32
U32 = mybir.dt.uint32
U16 = mybir.dt.uint16
U8 = mybir.dt.uint8
FP8X4 = mybir.dt.float8_e4m3fn_x4
ALU = mybir.AluOpType
COPY = mybir.ActivationFunctionType.Copy

P = 128
T = 2048
S = 512
PACK = 4
HALF = S // 2
SIXTEENTH = 0.0625
FLOPS = 4 * 2 * 512 * 512 * 512


def tile_picked_tricdflowbmaxbmed_none_po_kernel(
    tc, x_words, x_scales, w1_words, w1_scales, gs, offs, n1, n2, ca, cb, cd, n3, n4, n5, n6, n7, out_0, out_1, out_2
):
    nc = tc.nc
    with ExitStack() as ctx:
        keep = ctx.enter_context(tc.tile_pool(name="keep", bufs=1))
        psum = ctx.enter_context(tc.psum_pool(name="psum", bufs=1))

        def sbuf(name, shape, dtype, tag=None):
            return keep.tile(shape, dtype, name=name, tag=tag or name, align_bytes=64)

        def bank(number, name):
            return psum.tile([P, S], F32, name=name, tag="bank%d" % number)

        def load_list(name, source):
            tile = sbuf("list_" + name, [P, S // 16], U16)
            nc.sync.dma_start(tile[:], source)
            return tile

        def load_scale_rows(tile, source):
            for quadrant in range(4):
                nc.sync.dma_start(
                    tile[32 * quadrant : 32 * (quadrant + 1), :].bitcast(I32),
                    source[0, 4 * quadrant : 4 * quadrant + 4, :].bitcast(I32).partition_broadcast(8),
                )

        def entries(lst, start, count):
            return lst[:, start // 16 : (start + count) // 16]

        def dealt(ap):
            return ap.rearrange("p (t m) -> p m t", t=PACK)

        xs = sbuf("xs", [P, T], U8)
        ws = sbuf("ws", [P, S], U8)
        load_scale_rows(xs, x_scales)
        l_offs = load_list("offs", offs)
        l_ca = load_list("ca", ca)
        xw = sbuf("xw", [P, T], I32)
        nc.sync.dma_start(xw[:], x_words[0].rearrange("p c r -> p (c r)").bitcast(I32))
        ww = sbuf("ww", [P, S], I32)
        nc.sync.dma_start(ww[:], w1_words[0].rearrange("p c r -> p (c r)").bitcast(I32))
        load_scale_rows(ws, w1_scales)
        gain = sbuf("gain", [P, PACK], F32)
        nc.sync.dma_start(gain[:], gs.rearrange("(p t) o -> p (t o)", t=PACK))
        l_cb = load_list("cb", cb)
        l_n1 = load_list("n1", n1)
        l_n2 = load_list("n2", n2)
        l_cd = load_list("cd", cd)
        l_n4 = load_list("n4", n4)
        l_n3 = load_list("n3", n3)
        l_n5 = load_list("n5", n5)
        l_n7 = load_list("n7", n7)
        l_n6 = load_list("n6", n6)

        def pick_bytes(name, lst, tag=None):
            picked = sbuf(name + "_bytes", [P, S], U8, tag)
            nc.vector.tensor_copy(picked[:], xs[:].indirect(lst[:]))
            return picked

        def deal_bytes(name, source, tag=None):
            result = sbuf(name + "_dealt_bytes", [P, S], U8, tag)
            nc.vector.tensor_copy(
                result[:].rearrange("p (t m) -> p t m", t=PACK), source[:].rearrange("p (m t) -> p t m", t=PACK)
            )
            return result

        def pick_dealt_words(name, lst, tag=None):
            picked = sbuf(name + "_words", [P, S], U32, tag)
            nc.vector.tensor_copy(dealt(picked[:]), xw[:].bitcast(U32).indirect(lst[:]))
            return picked

        def product(out, words, scales, t, moving_words, moving_scales):
            cols = slice(P * t, P * (t + 1))
            nc.tensor.matmul_mx(
                out=out,
                lhsT=words[:, cols].bitcast(FP8X4),
                lhsT_scale=scales[:, cols],
                rhs=moving_words.bitcast(FP8X4),
                rhs_scale=moving_scales,
                start=True,
                stop=True,
            )

        xq_bytes = pick_bytes("xq", l_offs)
        xq_words = sbuf("xq_words", [P, S], U32)
        nc.vector.tensor_copy(xq_words[:], xw[:].bitcast(U32).indirect(l_offs[:]))
        w_words = sbuf("w_words", [P, S], I32)
        nc.vector.tensor_copy(dealt(w_words[:]), ww[:].rearrange("p (m t) -> p m t", t=PACK))
        w_scales = deal_bytes("w", ws)

        y = [sbuf("y%d" % t, [P, S], F32) for t in range(PACK)]
        y_banks = []
        for t in range(PACK):
            y_banks.append(bank(t, "y_bank%d" % t))
            product(y_banks[t][:], w_words, w_scales, t, xq_words[:], xq_bytes[:])

        ca_scales = deal_bytes("ca", pick_bytes("ca", l_ca), "ws")
        ca_words = pick_dealt_words("ca", l_ca, "ca_bytes")
        cb_bytes = pick_bytes("cb", l_cb)
        cb_words = pick_dealt_words("cb", l_cb)
        cb_scales = deal_bytes("cb", cb_bytes)

        z_words = sbuf("z_words", [P, S], U32)
        z_scales = sbuf("z_scales", [P, S], U8)
        a_win = [sbuf("a%d" % t, [P, 2 * S], F32) for t in range(PACK)]
        b_win = [sbuf("b%d" % t, [P, 3 * S if t else S], F32) for t in range(PACK)]
        q_win = [sbuf("q%d" % t, [P, 3 * S], F32) for t in range(PACK)]
        m_win = [sbuf("m%d" % t, [P, 2 * S], F32) for t in range(PACK)]
        low = sbuf("low", [P, PACK, S], F32)
        high = sbuf("high", [P, PACK, S], F32)
        pb = [sbuf("pb%d" % h, [P, PACK, HALF], F32) for h in range(2)]
        for t in range(PACK):
            pa = a_win[t][:, S : 2 * S]
            nc.scalar.activation(y[t][:], y_banks[t][:], COPY, scale=gain[:, t : t + 1])
            for h in range(2):
                nc.scalar.activation(
                    pa[:, HALF * h : HALF * (h + 1)], y[t][:].indirect(entries(l_n1, HALF * h, HALF)), COPY
                )
            nc.vector.tensor_tensor(high[:, t, :], y[t][:], pa, ALU.max)
            nc.vector.tensor_tensor(low[:, t, :], y[t][:], pa, ALU.min)
        for h in range(2):
            for t in range(PACK):
                nc.scalar.activation(pb[h][:, t, :], y[t][:].indirect(entries(l_n2, HALF * h, HALF)), COPY)
        ab_banks = {}
        a_plain = sbuf("a_plain", [P, S], F32)
        for h in range(2):
            cols = slice(HALF * h, HALF * (h + 1))
            capped = sbuf("capped%d" % h, [P, PACK, HALF], F32, "capped")
            for tiles in (slice(0, PACK - 1), slice(PACK - 1, PACK)):
                nc.vector.tensor_tensor(capped[:, tiles, :], high[:, tiles, cols], pb[h][:, tiles, :], ALU.min)
            z = sbuf("z%d" % h, [P, HALF, PACK], BF16)
            nc.vector.tensor_tensor(
                z[:].rearrange("p (c i) t -> p c t i", i=2),
                low[:, :, cols].rearrange("p t (c i) -> p c t i", i=2),
                capped[:].rearrange("p t (c i) -> p c t i", i=2),
                ALU.max,
            )
            nc.vector.quantize_mx(
                out=z_words[:, cols].bitcast(FP8X4), scales=z_scales[:, cols], in_=z[:].rearrange("p s t -> p (s t)")
            )
            for t in range(PACK):
                both = bank(4 * (1 - h) + t, "ab_bank%d_%d" % (h, t))
                ab_banks[(h, t)] = both
                product(both[:, 0:HALF], ca_words, ca_scales, t, z_words[:, cols], z_scales[:, cols])
                product(both[:, HALF:S], cb_words, cb_scales, t, z_words[:, cols], z_scales[:, cols])
                if h == 0:
                    nc.scalar.activation(a_win[t][:, cols], both[:, 0:HALF], COPY, scale=SIXTEENTH)
                    if t == 0:
                        nc.scalar.activation(a_plain[:, cols], both[:, 0:HALF], COPY, scale=SIXTEENTH)
                    nc.scalar.activation(b_win[t][:, cols], both[:, HALF:S], COPY, scale=SIXTEENTH)

        cd_bytes = pick_bytes("cd", l_cd, "capped")
        cd_words = pick_dealt_words("cd", l_cd, "low")
        cd_scales = deal_bytes("cd", cd_bytes)

        result = sbuf("result", [P, PACK, S], F32)
        out_rows = out_0.rearrange("(p t) s -> p t s", t=PACK)

        second = [sbuf("second%d" % t, [P, S], F32) for t in range(PACK)]
        q7 = [sbuf("q7_%d" % t, [P, S], F32) for t in range(PACK)]
        m6 = [sbuf("m6_%d" % t, [P, S], F32) for t in range(PACK)]
        larger = [sbuf("larger%d" % t, [P, S], F32) for t in range(PACK)]
        smaller = [sbuf("smaller%d" % t, [P, S], F32) for t in range(PACK)]
        whole = slice(0, S)

        def differences(t):
            both = ab_banks[(1, t)]
            nc.scalar.activation(a_win[t][:, HALF:S], both[:, 0:HALF], COPY, scale=SIXTEENTH)
            if t == 0:
                nc.scalar.activation(a_plain[:, HALF:S], both[:, 0:HALF], COPY, scale=SIXTEENTH)
                nc.scalar.activation(b_win[t][:, HALF:S], both[:, HALF:S], COPY, scale=SIXTEENTH)
                nc.vector.tensor_tensor(
                    q_win[t][:, 2 * S : 3 * S], a_win[t][:].indirect(l_n3[:]), a_plain[:], ALU.subtract
                )
                nc.vector.tensor_tensor(q_win[t][:, S : 2 * S], a_win[t][:].indirect(l_n4[:]), a_plain[:], ALU.subtract)
            else:
                nc.scalar.activation(b_win[t][:, S : 2 * S], a_win[t][:].indirect(l_n4[:]), COPY)
                nc.scalar.activation(b_win[t][:, 2 * S : 3 * S], a_win[t][:].indirect(l_n3[:]), COPY)
                nc.scalar.activation(b_win[t][:, HALF:S], both[:, HALF:S], COPY, scale=SIXTEENTH)
                nc.vector.tensor_tensor(
                    q_win[t][:, S : 3 * S].rearrange("p (k s) -> p k s", k=2),
                    b_win[t][:, S : 3 * S].rearrange("p (k s) -> p k s", k=2),
                    a_win[t][:, 0:S].unsqueeze(1).to_broadcast([P, 2, S]),
                    ALU.subtract,
                )

        def terms(t):
            nc.vector.tensor_tensor(m_win[t][:, S : 2 * S], b_win[t][:, 0:S], q_win[t][:, 2 * S : 3 * S], ALU.mult)
            width = S if t else HALF
            for start in range(0, S, width):
                nc.vector.tensor_tensor(
                    second[t][:, start : start + width],
                    b_win[t][:].indirect(entries(l_n5, start, width)),
                    q_win[t][:, S + start : S + start + width],
                    ALU.mult,
                )

        def join_terms(t):
            nc.vector.scalar_tensor_tensor(
                m_win[t][:, 0:S], second[t][:], 0.5, m_win[t][:, S : 2 * S], ALU.mult, ALU.add
            )

        def score(t):
            q_bank = bank(4 + t, "q_bank%d" % t)
            product(q_bank[:], cd_words, cd_scales, t, z_words[:], z_scales[:])
            nc.scalar.activation(q_win[t][:, 0:S], q_bank[:], COPY, scale=SIXTEENTH)
            nc.scalar.activation(q7[t][:], q_win[t][:].indirect(l_n7[:]), COPY)

        def fetch_m6(t, cols):
            nc.scalar.activation(
                m6[t][:, cols], m_win[t][:].indirect(entries(l_n6, cols.start, cols.stop - cols.start)), COPY
            )

        def take_larger(t):
            nc.vector.tensor_tensor(larger[t][:], m_win[t][:, 0:S], q7[t][:], ALU.max)

        def take_smaller(t, cols):
            nc.vector.tensor_tensor(smaller[t][:, cols], m6[t][:, cols], q_win[t][:, cols], ALU.min)

        def finish(t, cols):
            nc.vector.tensor_tensor(result[:, t, cols], larger[t][:, cols], smaller[t][:, cols], ALU.subtract)
            nc.sync.dma_start(out_rows[:, t, cols], result[:, t, cols])

        for t in range(PACK):
            done = t - 2
            differences(t)
            if done >= 0:
                fetch_m6(done, whole)
                take_larger(done)
            terms(t)
            if done >= 0:
                take_smaller(done, whole)
            join_terms(t)
            if done >= 0:
                finish(done, whole)
            if t >= 1:
                score(t - 1)

        last = PACK - 1
        halves = (slice(0, HALF), slice(HALF, S))
        fetch_m6(last - 1, whole)
        score(last)
        take_larger(last - 1)
        take_larger(last)
        for cols in halves:
            fetch_m6(last, cols)
            for t in (last - 1, last):
                take_smaller(t, cols)
            for t in (last - 1, last):
                finish(t, cols)

        out_words = sbuf("out_words", [P, S], U32)
        out_scales = sbuf("out_scales", [P, S], U8)
        words_hbm = out_1[0].rearrange("p c r -> p (c r)").bitcast(I32)
        rounded = [sbuf("rounded%d" % h, [P, HALF, PACK], BF16) for h in range(2)]
        for h, cols in enumerate(halves):
            target = rounded[h][:].rearrange("p (c i) t -> p c t i", i=2)
            source = result[:, :, cols].rearrange("p t (c i) -> p c t i", i=2)
            if h == 0:
                nc.scalar.copy(target, source)
            else:
                nc.vector.tensor_copy(target, source)
        for h, cols in enumerate(halves):
            nc.vector.quantize_mx(
                out=out_words[:, cols].bitcast(FP8X4),
                scales=out_scales[:, cols],
                in_=rounded[h][:].rearrange("p s t -> p (s t)"),
            )
            nc.sync.dma_start(words_hbm[:, cols], out_words[:, cols].bitcast(I32))
        for quadrant in range(4):
            (nc.scalar if quadrant % 2 else nc.sync).dma_start(
                out_2[0, 4 * quadrant : 4 * quadrant + 4, :].bitcast(I32),
                out_scales[32 * quadrant : 32 * quadrant + 4, :].bitcast(I32),
            )
